import numpy as np
import ml_dtypes


def mxq(x, axis, fmt="e4m3"):
    dtype, down = {"e4m3": (ml_dtypes.float8_e4m3fn, 7), "e5m2": (ml_dtypes.float8_e5m2, 14)}[fmt]
    v = np.moveaxis(np.asarray(x, np.float32).astype(ml_dtypes.bfloat16).astype(np.float64), axis, -1)
    blocks = v.reshape(v.shape[:-1] + (-1, 32))
    amax = np.abs(blocks).max(-1, keepdims=True)
    byte = np.maximum(np.where(amax > 0, np.frexp(amax)[1] - 1 + 127, 0) - down, 1)
    scale = np.exp2(byte - 127.0)
    codes = (blocks / scale).astype(np.float32).astype(dtype).astype(np.float64)
    return np.moveaxis((codes * scale).reshape(v.shape), -1, axis)


WIDE = False


def mx_kscale(k):
    if not WIDE:
        return np.ones(k)
    levels = np.array([10, -10, 5, -5, 0])
    if k % 512:
        return np.exp2(np.random.permutation(np.resize(levels, k // 32))).repeat(32)
    a = np.empty((k // 512, 16))
    for p in range(k // 512):
        a[p, :8] = np.random.permutation(np.resize(levels, 8))
        for g in range(8):
            far = levels[np.abs(levels - a[p, g]) >= 10]
            a[p, g + 8] = far[np.random.randint(len(far))]
    return np.exp2(a.ravel()).repeat(32)


def f64(x):
    return np.asarray(x).astype(np.float64)


def striped(idx):
    return np.tile(np.asarray(idx).reshape(-1, 16).T, (8, 1)).astype(np.uint16)


def unstriped(offs):
    return offs[:16].T.reshape(-1).astype(np.int64)


E2M1 = np.array([0.0, 0.5, 1.0, 1.5, 2.0, 3.0, 4.0, 6.0, -0.0, -0.5, -1.0, -1.5, -2.0, -3.0, -4.0, -6.0])


def pack_weight(w, fmt):
    k, n = w.shape
    w = f64(np.asarray(w, np.float32).astype(ml_dtypes.bfloat16)).reshape(k // 32, 32, n)
    amax = np.abs(w).max(1)
    if fmt == "e4m3":
        byte = np.frexp(amax)[1] - 1 + 127 - 7
    else:
        mant, ex = np.frexp(amax / 6.0)
        byte = np.where(mant > 0.5, ex, ex - 1) + 127
    byte = np.clip(np.where(amax > 0, byte, 1), 1, 254)
    scaled = (w * np.exp2(127.0 - byte)[:, None, :]).reshape(k, n).astype(np.float32)
    by_word = np.ascontiguousarray(scaled.reshape(k // 512, 128, 4, n).transpose(0, 1, 3, 2))
    if fmt == "e4m3":
        words = by_word.astype(ml_dtypes.float8_e4m3fn).view(np.uint8)
    else:
        c = by_word.astype(ml_dtypes.float4_e2m1fn).view(np.uint8) & 0xF
        words = (c[..., 0::2] | (c[..., 1::2] << 4)).reshape(k // 512, 128, 2 * n)
    return np.ascontiguousarray(words), np.ascontiguousarray(byte.astype(np.uint8).reshape(k // 512, 16, n))


def unpack_weight(words, scales, fmt):
    g, _, n = scales.shape
    words = np.ascontiguousarray(words).reshape(g, 128, n, -1)
    if fmt == "e4m3":
        vals = words.view(ml_dtypes.float8_e4m3fn).astype(np.float64)
    else:
        nib = np.empty((g, 128, n, 4), np.uint8)
        nib[..., 0::2] = words & 0xF
        nib[..., 1::2] = words >> 4
        vals = E2M1[nib]
    vals = vals * np.repeat(np.exp2(scales.astype(np.float64) - 127.0), 8, axis=1)[..., None]
    return vals.transpose(0, 1, 3, 2).reshape(g * 512, n)


D, K, T, I, J, Q = 512, 512, 2048, 1024, 512, 128


def setup_inputs():
    n = np.random.standard_normal
    idx = np.random.permutation(T)[:I]
    idx2 = np.random.randint(0, I, J)
    idx3 = np.random.randint(0, I, J)
    idx4 = np.random.randint(0, I, J)
    fd = mx_kscale(D)
    fk = mx_kscale(K)
    etp = pack_weight(n((D, T)) / fd[:, None], "e2m1")
    edp = pack_weight(n((K, T)) / fk[:, None], "e4m3")
    return {
        "ht": (n((D, Q)) * 0.6 / np.sqrt(D) * fd[:, None]).astype(np.float32),
        "hd": (n((K, Q)) * 0.6 / np.sqrt(K) * fk[:, None]).astype(np.float32),
        "et_words": etp[0],
        "et_scales": etp[1],
        "ed_words": edp[0],
        "ed_scales": edp[1],
        "l1": (np.random.uniform(7.0, 7.3, (Q, 1))).astype(np.float32),
        "l2": (np.random.uniform(7.0, 7.3, (Q, 1))).astype(np.float32),
        "offs": striped(idx),
        "offs2": striped(idx2),
        "offs3": striped(idx3),
        "offs4": striped(idx4),
    }


def reference(ht, hd, et_words, et_scales, ed_words, ed_scales, l1, l2, offs, offs2, offs3, offs4):
    idx = unstriped(offs)
    idx2 = unstriped(offs2)
    idx3 = unstriped(offs3)
    idx4 = unstriped(offs4)
    etu = unpack_weight(et_words, et_scales, "e2m1")
    edu = unpack_weight(ed_words, ed_scales, "e4m3")
    htq = mxq(f64(ht), 0, "e4m3")
    etidxg = etu[:, idx]
    a = htq.T @ etidxg
    hdq = mxq(f64(hd), 0, "e4m3")
    edidxg = edu[:, idx]
    b = hdq.T @ edidxg
    r = np.minimum(np.exp(a - f64(l1) - b + f64(l2)), 1.0)
    y = r[:, idx2] * (r[:, idx3] * (r[:, idx4] + 1.0) + 1.0)
    return y

@@ -1,0 +1,126 @@
+from contextlib import ExitStack
+
+import concourse.mybir as mybir
+
+D, T, I, J, Q = 512, 2048, 1024, 512, 128
+FLOPS = 2 * 2 * D * Q * I
+
+F32 = mybir.dt.float32
+BF16 = mybir.dt.bfloat16
+I32 = mybir.dt.int32
+U32 = mybir.dt.uint32
+U16 = mybir.dt.uint16
+U8 = mybir.dt.uint8
+FP8X4 = mybir.dt.float8_e4m3fn_x4
+FP4X4 = mybir.dt.float4_e2m1fn_x4
+ACT = mybir.ActivationFunctionType
+ALU = mybir.AluOpType
+
+P = 128
+PACK = 4
+PER_COL = 16
+
+
+def listed(window, offsets, first, last):
+    return window[:].indirect(offsets[:, first // PER_COL : last // PER_COL])
+
+
+def tile_attend_acceptedlength_kernel(
+    tc, ht, hd, et_words, et_scales, ed_words, ed_scales, l1, l2, offs, offs2, offs3, offs4, out
+):
+    nc = tc.nc
+    with ExitStack() as ctx:
+        sb = ctx.enter_context(tc.tile_pool(name="sb", bufs=1))
+        psum = ctx.enter_context(tc.psum_pool(name="psum", bufs=1))
+
+        nodes = sb.tile([P, I // PER_COL], U16, name="nodes")
+        first_node = sb.tile([P, J // PER_COL], U16, name="first_node")
+        second_node = sb.tile([P, J // PER_COL], U16, name="second_node")
+        third_node = sb.tile([P, J // PER_COL], U16, name="third_node")
+        et_w = sb.tile([P, T], U16, name="et_w", align_bytes=64)
+        ed_w = sb.tile([P, T], U32, name="ed_w", align_bytes=64)
+        et_s = sb.tile([P, T], U8, name="et_s", align_bytes=64)
+        ed_s = sb.tile([P, T], U8, name="ed_s", align_bytes=64)
+        ht_raw = sb.tile([P, PACK, Q], F32, name="ht_raw")
+        hd_raw = sb.tile([P, PACK, Q], F32, name="hd_raw")
+        l1_col = sb.tile([P, 1], F32, name="l1_col")
+        l2_col = sb.tile([P, 1], F32, name="l2_col")
+        ratio = sb.tile([P, 2 * I], F32, name="ratio", align_bytes=64)
+
+        nc.vector.memset(et_s[:].bitcast(I32), 0)
+        nc.vector.memset(ed_s[:].bitcast(I32), 0)
+        nc.vector.memset(ratio[:, I:], 0.0)
+
+        nc.sync.dma_start(nodes[:], offs)
+        nc.sync.dma_start(et_w[:].bitcast(I32), et_words[0].bitcast(I32))
+        nc.sync.dma_start(ed_w[:].bitcast(I32), ed_words[0].rearrange("p n t -> p (n t)").bitcast(I32))
+        nc.sync.dma_start(ht_raw[:], ht.rearrange("(p j) q -> p j q", j=PACK))
+        nc.sync.dma_start(hd_raw[:], hd.rearrange("(p j) q -> p j q", j=PACK))
+        for plane, rows in ((et_s, et_scales), (ed_s, ed_scales)):
+            for quad in range(4):
+                nc.sync.dma_start(
+                    plane[32 * quad : 32 * quad + 4, :].bitcast(I32),
+                    rows[0, 4 * quad : 4 * quad + 4, :].bitcast(I32),
+                )
+        nc.sync.dma_start(l1_col[:], l1)
+        nc.sync.dma_start(l2_col[:], l2)
+        nc.sync.dma_start(third_node[:], offs4)
+        nc.sync.dma_start(second_node[:], offs3)
+        nc.sync.dma_start(first_node[:], offs2)
+
+        h_bf = sb.tile([P, 2, Q, PACK], BF16, name="h_bf", align_bytes=64)
+        nc.scalar.activation(h_bf[:, 0], ht_raw[:].rearrange("p j q -> p q j"), ACT.Copy)
+        nc.scalar.activation(h_bf[:, 1], hd_raw[:].rearrange("p j q -> p q j"), ACT.Copy, scale=-1.0)
+        gap = sb.tile([P, 1], F32, name="gap")
+        nc.scalar.activation(gap[:], l2_col[:], ACT.Identity, bias=l1_col[:], scale=-1.0)
+
+        et_wg = sb.tile([P, I], U16, name="et_wg", align_bytes=64)
+        ed_wg = sb.tile([P, I], U32, name="ed_wg", align_bytes=64)
+        et_sg = sb.tile([P, I], U8, name="et_sg", align_bytes=64)
+        ed_sg = sb.tile([P, I], U8, name="ed_sg", align_bytes=64)
+        h_w = sb.tile([P, 2 * Q], U32, name="h_w", align_bytes=64)
+        h_s = sb.tile([P, 2 * Q], U8, name="h_s", align_bytes=64)
+
+        for lo, hi in ((0, 512), (512, 1024)):
+            nc.vector.tensor_copy(et_wg[:, lo:hi], listed(et_w, nodes, lo, hi))
+        nc.vector.tensor_copy(ed_wg[:], listed(ed_w, nodes, 0, I))
+        nc.vector.quantize_mx(
+            out=h_w[:].bitcast(FP8X4), scales=h_s[:], in_=h_bf[:].rearrange("p a q j -> p (a q j)")
+        )
+        chunks = ((0, 512), (512, 768), (768, 1024))
+        for lo, hi in chunks:
+            nc.vector.tensor_copy(et_sg[:, lo:hi], listed(et_s, nodes, lo, hi))
+            nc.vector.tensor_copy(ed_sg[:, lo:hi], listed(ed_s, nodes, lo, hi))
+
+        groups = ((0, 512), (512, 640), (640, 768), (768, 896), (896, 1024))
+        banks = [psum.tile([P, hi - lo], F32, name="bank%d" % lo) for lo, hi in groups]
+        short = sb.tile([P, I], F32, name="short")
+        for clo, chi in chunks:
+            mine = [(bank, lo, hi) for bank, (lo, hi) in zip(banks, groups) if clo <= lo < chi]
+            for bank, lo, hi in mine:
+                nc.tensor.matmul_mx(
+                    out=bank[:], lhsT=h_w[:, :Q].bitcast(FP8X4), lhsT_scale=h_s[:, :Q],
+                    rhs=et_wg[:, lo:hi].bitcast(FP4X4), rhs_scale=et_sg[:, lo:hi], start=True, stop=False,
+                )
+            for bank, lo, hi in mine:
+                nc.tensor.matmul_mx(
+                    out=bank[:], lhsT=h_w[:, Q:].bitcast(FP8X4), lhsT_scale=h_s[:, Q:],
+                    rhs=ed_wg[:, lo:hi].bitcast(FP8X4), rhs_scale=ed_sg[:, lo:hi], start=False, stop=True,
+                )
+            for bank, lo, hi in mine:
+                nc.scalar.activation(short[:, lo:hi], bank[:], ACT.Relu, bias=gap[:], scale=-1.0)
+            for bank, lo, hi in mine:
+                nc.scalar.activation(ratio[:, lo:hi], short[:, lo:hi], ACT.Exp, scale=-1.0)
+
+        inner = sb.tile([P, J], F32, name="inner")
+        middle = sb.tile([P, J], F32, name="middle")
+        outer = sb.tile([P, J], F32, name="outer")
+        length = sb.tile([P, J], F32, name="length")
+        nc.vector.tensor_scalar(inner[:], listed(ratio, third_node, 0, J), 1.0, 1.0, ALU.mult, ALU.add)
+        halves = ((0, 256), (256, 512))
+        for lo, hi in halves:
+            nc.vector.tensor_tensor(middle[:, lo:hi], listed(ratio, second_node, lo, hi), inner[:, lo:hi], ALU.mult)
+            nc.scalar.activation(outer[:, lo:hi], middle[:, lo:hi], ACT.Copy, bias=1.0)
+        for lo, hi in halves:
+            nc.vector.tensor_tensor(length[:, lo:hi], listed(ratio, first_node, lo, hi), outer[:, lo:hi], ALU.mult)
+            nc.sync.dma_start(out[:, lo:hi], length[:, lo:hi])

@@ -19,6 +19,8 @@ ALU = mybir.AluOpType
 P = 128
 PACK = 4
 PER_COL = 16
+CHUNK = 256
+GROUP = 128
 
 
 def listed(window, offsets, first, last):
@@ -31,6 +33,7 @@ def tile_attend_acceptedlength_kernel(
     nc = tc.nc
     with ExitStack() as ctx:
         sb = ctx.enter_context(tc.tile_pool(name="sb", bufs=1))
+        ring = ctx.enter_context(tc.tile_pool(name="ring", bufs=2))
         psum = ctx.enter_context(tc.psum_pool(name="psum", bufs=1))
 
         nodes = sb.tile([P, I // PER_COL], U16, name="nodes")
@@ -51,13 +54,13 @@ def tile_attend_acceptedlength_kernel(
         nc.vector.memset(ed_s[:].bitcast(I32), 0)
         nc.vector.memset(ratio[:, I:], 0.0)
 
-        nc.sync.dma_start(nodes[:], offs)
         nc.sync.dma_start(et_w[:].bitcast(I32), et_words[0].bitcast(I32))
+        nc.sync.dma_start(nodes[:], offs)
         nc.sync.dma_start(ed_w[:].bitcast(I32), ed_words[0].rearrange("p n t -> p (n t)").bitcast(I32))
         nc.sync.dma_start(ht_raw[:], ht.rearrange("(p j) q -> p j q", j=PACK))
         nc.sync.dma_start(hd_raw[:], hd.rearrange("(p j) q -> p j q", j=PACK))
-        for plane, rows in ((et_s, et_scales), (ed_s, ed_scales)):
-            for quad in range(4):
+        for quad in range(4):
+            for plane, rows in ((et_s, et_scales), (ed_s, ed_scales)):
                 nc.sync.dma_start(
                     plane[32 * quad : 32 * quad + 4, :].bitcast(I32),
                     rows[0, 4 * quad : 4 * quad + 4, :].bitcast(I32),
@@ -87,30 +90,36 @@ def tile_attend_acceptedlength_kernel(
         nc.vector.quantize_mx(
             out=h_w[:].bitcast(FP8X4), scales=h_s[:], in_=h_bf[:].rearrange("p a q j -> p (a q j)")
         )
-        chunks = ((0, 512), (512, 768), (768, 1024))
-        for lo, hi in chunks:
-            nc.vector.tensor_copy(et_sg[:, lo:hi], listed(et_s, nodes, lo, hi))
-            nc.vector.tensor_copy(ed_sg[:, lo:hi], listed(ed_s, nodes, lo, hi))
+        nc.vector.tensor_copy(et_sg[:], listed(et_s, nodes, 0, I))
+        for lo in range(0, I, CHUNK):
+            nc.vector.tensor_copy(ed_sg[:, lo : lo + CHUNK], listed(ed_s, nodes, lo, lo + CHUNK))
 
-        groups = ((0, 512), (512, 640), (640, 768), (768, 896), (896, 1024))
-        banks = [psum.tile([P, hi - lo], F32, name="bank%d" % lo) for lo, hi in groups]
-        short = sb.tile([P, I], F32, name="short")
-        for clo, chi in chunks:
-            mine = [(bank, lo, hi) for bank, (lo, hi) in zip(banks, groups) if clo <= lo < chi]
-            for bank, lo, hi in mine:
-                nc.tensor.matmul_mx(
-                    out=bank[:], lhsT=h_w[:, :Q].bitcast(FP8X4), lhsT_scale=h_s[:, :Q],
-                    rhs=et_wg[:, lo:hi].bitcast(FP4X4), rhs_scale=et_sg[:, lo:hi], start=True, stop=False,
-                )
-            for bank, lo, hi in mine:
-                nc.tensor.matmul_mx(
-                    out=bank[:], lhsT=h_w[:, Q:].bitcast(FP8X4), lhsT_scale=h_s[:, Q:],
-                    rhs=ed_wg[:, lo:hi].bitcast(FP8X4), rhs_scale=ed_sg[:, lo:hi], start=False, stop=True,
-                )
-            for bank, lo, hi in mine:
-                nc.scalar.activation(short[:, lo:hi], bank[:], ACT.Relu, bias=gap[:], scale=-1.0)
-            for bank, lo, hi in mine:
-                nc.scalar.activation(ratio[:, lo:hi], short[:, lo:hi], ACT.Exp, scale=-1.0)
+        banks = [psum.tile([P, GROUP], F32, name="bank%d" % g) for g in range(I // GROUP)]
+        for g, bank in enumerate(banks):
+            cols = slice(g * GROUP, (g + 1) * GROUP)
+            nc.tensor.matmul_mx(
+                out=bank[:], lhsT=h_w[:, :Q].bitcast(FP8X4), lhsT_scale=h_s[:, :Q],
+                rhs=et_wg[:, cols].bitcast(FP4X4), rhs_scale=et_sg[:, cols], start=True, stop=False,
+            )
+        for g, bank in enumerate(banks):
+            cols = slice(g * GROUP, (g + 1) * GROUP)
+            nc.tensor.matmul_mx(
+                out=bank[:], lhsT=h_w[:, Q:].bitcast(FP8X4), lhsT_scale=h_s[:, Q:],
+                rhs=ed_wg[:, cols].bitcast(FP8X4), rhs_scale=ed_sg[:, cols], start=False, stop=True,
+            )
+
+        for lo in range(0, I, CHUNK):
+            log_ratio = ring.tile([P, CHUNK], F32, name="log_ratio")
+            parts = [(banks[(lo + c) // GROUP], c) for c in range(0, CHUNK, GROUP)]
+            if lo + CHUNK < I:
+                for bank, c in parts:
+                    nc.scalar.activation(log_ratio[:, c : c + GROUP], bank[:], ACT.Relu, bias=gap[:], scale=-1.0)
+                nc.scalar.activation(ratio[:, lo : lo + CHUNK], log_ratio[:], ACT.Exp, scale=-1.0)
+            else:
+                for bank, c in parts:
+                    nc.vector.tensor_scalar(log_ratio[:, c : c + GROUP], bank[:], gap[:], 0.0, ALU.subtract, ALU.min)
+                for bank, c in parts:
+                    nc.scalar.activation(ratio[:, lo + c : lo + c + GROUP], log_ratio[:, c : c + GROUP], ACT.Exp)
 
         inner = sb.tile([P, J], F32, name="inner")
         middle = sb.tile([P, J], F32, name="middle")

@@ -21,10 +21,11 @@ PACK = 4
 PER_COL = 16
 CHUNK = 256
 GROUP = 128
+PIECE = 128
 
 
 def listed(window, offsets, first, last):
-    return window[:].indirect(offsets[:, first // PER_COL : last // PER_COL])
+    return window.indirect(offsets[:, first // PER_COL : last // PER_COL])
 
 
 def tile_attend_acceptedlength_kernel(
@@ -57,25 +58,25 @@ def tile_attend_acceptedlength_kernel(
         nc.sync.dma_start(et_w[:].bitcast(I32), et_words[0].bitcast(I32))
         nc.sync.dma_start(nodes[:], offs)
         nc.sync.dma_start(ed_w[:].bitcast(I32), ed_words[0].rearrange("p n t -> p (n t)").bitcast(I32))
+        nc.sync.dma_start(third_node[:], offs4)
+        nc.sync.dma_start(second_node[:], offs3)
+        nc.sync.dma_start(first_node[:], offs2)
+        nc.sync.dma_start(l1_col[:], l1)
+        nc.sync.dma_start(l2_col[:], l2)
         nc.sync.dma_start(ht_raw[:], ht.rearrange("(p j) q -> p j q", j=PACK))
         nc.sync.dma_start(hd_raw[:], hd.rearrange("(p j) q -> p j q", j=PACK))
-        for quad in range(4):
-            for plane, rows in ((et_s, et_scales), (ed_s, ed_scales)):
+        for plane, rows in ((et_s, et_scales), (ed_s, ed_scales)):
+            for quad in range(4):
                 nc.sync.dma_start(
                     plane[32 * quad : 32 * quad + 4, :].bitcast(I32),
                     rows[0, 4 * quad : 4 * quad + 4, :].bitcast(I32),
                 )
-        nc.sync.dma_start(l1_col[:], l1)
-        nc.sync.dma_start(l2_col[:], l2)
-        nc.sync.dma_start(third_node[:], offs4)
-        nc.sync.dma_start(second_node[:], offs3)
-        nc.sync.dma_start(first_node[:], offs2)
 
         h_bf = sb.tile([P, 2, Q, PACK], BF16, name="h_bf", align_bytes=64)
         nc.scalar.activation(h_bf[:, 0], ht_raw[:].rearrange("p j q -> p q j"), ACT.Copy)
         nc.scalar.activation(h_bf[:, 1], hd_raw[:].rearrange("p j q -> p q j"), ACT.Copy, scale=-1.0)
         gap = sb.tile([P, 1], F32, name="gap")
-        nc.scalar.activation(gap[:], l2_col[:], ACT.Identity, bias=l1_col[:], scale=-1.0)
+        nc.gpsimd.tensor_tensor(gap[:], l1_col[:], l2_col[:], ALU.subtract)
 
         et_wg = sb.tile([P, I], U16, name="et_wg", align_bytes=64)
         ed_wg = sb.tile([P, I], U32, name="ed_wg", align_bytes=64)
@@ -85,14 +86,14 @@ def tile_attend_acceptedlength_kernel(
         h_s = sb.tile([P, 2 * Q], U8, name="h_s", align_bytes=64)
 
         for lo, hi in ((0, 512), (512, 1024)):
-            nc.vector.tensor_copy(et_wg[:, lo:hi], listed(et_w, nodes, lo, hi))
-        nc.vector.tensor_copy(ed_wg[:], listed(ed_w, nodes, 0, I))
+            nc.vector.tensor_copy(et_wg[:, lo:hi], listed(et_w[:], nodes, lo, hi))
+        nc.vector.tensor_copy(ed_wg[:], listed(ed_w[:], nodes, 0, I))
         nc.vector.quantize_mx(
             out=h_w[:].bitcast(FP8X4), scales=h_s[:], in_=h_bf[:].rearrange("p a q j -> p (a q j)")
         )
-        nc.vector.tensor_copy(et_sg[:], listed(et_s, nodes, 0, I))
+        nc.vector.tensor_copy(et_sg[:], listed(et_s[:], nodes, 0, I))
         for lo in range(0, I, CHUNK):
-            nc.vector.tensor_copy(ed_sg[:, lo : lo + CHUNK], listed(ed_s, nodes, lo, lo + CHUNK))
+            nc.vector.tensor_copy(ed_sg[:, lo : lo + CHUNK], listed(ed_s[:], nodes, lo, lo + CHUNK))
 
         banks = [psum.tile([P, GROUP], F32, name="bank%d" % g) for g in range(I // GROUP)]
         for g, bank in enumerate(banks):
@@ -123,13 +124,24 @@ def tile_attend_acceptedlength_kernel(
 
         inner = sb.tile([P, J], F32, name="inner")
         middle = sb.tile([P, J], F32, name="middle")
-        outer = sb.tile([P, J], F32, name="outer")
+        outer = sb.tile([P, J - PIECE], F32, name="outer")
+        first_tail = sb.tile([P, PIECE], F32, name="first_tail")
         length = sb.tile([P, J], F32, name="length")
-        nc.vector.tensor_scalar(inner[:], listed(ratio, third_node, 0, J), 1.0, 1.0, ALU.mult, ALU.add)
-        halves = ((0, 256), (256, 512))
-        for lo, hi in halves:
-            nc.vector.tensor_tensor(middle[:, lo:hi], listed(ratio, second_node, lo, hi), inner[:, lo:hi], ALU.mult)
-            nc.scalar.activation(outer[:, lo:hi], middle[:, lo:hi], ACT.Copy, bias=1.0)
-        for lo, hi in halves:
-            nc.vector.tensor_tensor(length[:, lo:hi], listed(ratio, first_node, lo, hi), outer[:, lo:hi], ALU.mult)
+        tail = J - PIECE
+        nc.vector.tensor_scalar(inner[:], listed(ratio[:], third_node, 0, J), 1.0, 1.0, ALU.mult, ALU.add)
+        nc.vector.tensor_copy(first_tail[:], listed(ratio[:, :I], first_node, tail, J))
+        for lo in range(0, J, PIECE):
+            cols = slice(lo, lo + PIECE)
+            nc.vector.tensor_tensor(
+                middle[:, cols], listed(ratio[:], second_node, lo, lo + PIECE), inner[:, cols], ALU.mult
+            )
+            if lo < tail:
+                nc.scalar.activation(outer[:, cols], middle[:, cols], ACT.Copy, bias=1.0)
+        for lo in range(0, tail, PIECE):
+            cols = slice(lo, lo + PIECE)
+            nc.vector.tensor_tensor(
+                length[:, cols], listed(ratio[:], first_node, lo, lo + PIECE), outer[:, cols], ALU.mult
+            )
+        nc.vector.scalar_tensor_tensor(length[:, tail:], middle[:, tail:], 1.0, first_tail[:], ALU.add, ALU.mult)
+        for lo, hi in ((0, 256), (256, 384), (384, 512)):
             nc.sync.dma_start(out[:, lo:hi], length[:, lo:hi])

@@ -58,25 +58,25 @@ def tile_attend_acceptedlength_kernel(
         nc.sync.dma_start(et_w[:].bitcast(I32), et_words[0].bitcast(I32))
         nc.sync.dma_start(nodes[:], offs)
         nc.sync.dma_start(ed_w[:].bitcast(I32), ed_words[0].rearrange("p n t -> p (n t)").bitcast(I32))
-        nc.sync.dma_start(third_node[:], offs4)
-        nc.sync.dma_start(second_node[:], offs3)
-        nc.sync.dma_start(first_node[:], offs2)
-        nc.sync.dma_start(l1_col[:], l1)
-        nc.sync.dma_start(l2_col[:], l2)
         nc.sync.dma_start(ht_raw[:], ht.rearrange("(p j) q -> p j q", j=PACK))
         nc.sync.dma_start(hd_raw[:], hd.rearrange("(p j) q -> p j q", j=PACK))
-        for plane, rows in ((et_s, et_scales), (ed_s, ed_scales)):
-            for quad in range(4):
+        for quad in range(4):
+            for plane, rows in ((et_s, et_scales), (ed_s, ed_scales)):
                 nc.sync.dma_start(
                     plane[32 * quad : 32 * quad + 4, :].bitcast(I32),
                     rows[0, 4 * quad : 4 * quad + 4, :].bitcast(I32),
                 )
+        nc.sync.dma_start(l1_col[:], l1)
+        nc.sync.dma_start(l2_col[:], l2)
+        nc.sync.dma_start(third_node[:], offs4)
+        nc.sync.dma_start(second_node[:], offs3)
+        nc.sync.dma_start(first_node[:], offs2)
 
         h_bf = sb.tile([P, 2, Q, PACK], BF16, name="h_bf", align_bytes=64)
         nc.scalar.activation(h_bf[:, 0], ht_raw[:].rearrange("p j q -> p q j"), ACT.Copy)
         nc.scalar.activation(h_bf[:, 1], hd_raw[:].rearrange("p j q -> p q j"), ACT.Copy, scale=-1.0)
         gap = sb.tile([P, 1], F32, name="gap")
-        nc.gpsimd.tensor_tensor(gap[:], l1_col[:], l2_col[:], ALU.subtract)
+        nc.scalar.activation(gap[:], l2_col[:], ACT.Identity, bias=l1_col[:], scale=-1.0)
 
         et_wg = sb.tile([P, I], U16, name="et_wg", align_bytes=64)
         ed_wg = sb.tile([P, I], U32, name="ed_wg", align_bytes=64)

from contextlib import ExitStack

import concourse.mybir as mybir

D, T, I, J, Q = 512, 2048, 1024, 512, 128
FLOPS = 2 * 2 * D * Q * I

F32 = mybir.dt.float32
BF16 = mybir.dt.bfloat16
I32 = mybir.dt.int32
U32 = mybir.dt.uint32
U16 = mybir.dt.uint16
U8 = mybir.dt.uint8
FP8X4 = mybir.dt.float8_e4m3fn_x4
FP4X4 = mybir.dt.float4_e2m1fn_x4
ACT = mybir.ActivationFunctionType
ALU = mybir.AluOpType

P = 128
PACK = 4
PER_COL = 16
CHUNK = 256
GROUP = 128
PIECE = 128


def listed(window, offsets, first, last):
    return window.indirect(offsets[:, first // PER_COL : last // PER_COL])


def tile_attend_acceptedlength_kernel(
    tc, ht, hd, et_words, et_scales, ed_words, ed_scales, l1, l2, offs, offs2, offs3, offs4, out
):
    nc = tc.nc
    with ExitStack() as ctx:
        sb = ctx.enter_context(tc.tile_pool(name="sb", bufs=1))
        ring = ctx.enter_context(tc.tile_pool(name="ring", bufs=2))
        psum = ctx.enter_context(tc.psum_pool(name="psum", bufs=1))

        nodes = sb.tile([P, I // PER_COL], U16, name="nodes")
        first_node = sb.tile([P, J // PER_COL], U16, name="first_node")
        second_node = sb.tile([P, J // PER_COL], U16, name="second_node")
        third_node = sb.tile([P, J // PER_COL], U16, name="third_node")
        et_w = sb.tile([P, T], U16, name="et_w", align_bytes=64)
        ed_w = sb.tile([P, T], U32, name="ed_w", align_bytes=64)
        et_s = sb.tile([P, T], U8, name="et_s", align_bytes=64)
        ed_s = sb.tile([P, T], U8, name="ed_s", align_bytes=64)
        ht_raw = sb.tile([P, PACK, Q], F32, name="ht_raw")
        hd_raw = sb.tile([P, PACK, Q], F32, name="hd_raw")
        l1_col = sb.tile([P, 1], F32, name="l1_col")
        l2_col = sb.tile([P, 1], F32, name="l2_col")
        ratio = sb.tile([P, 2 * I], F32, name="ratio", align_bytes=64)

        nc.vector.memset(et_s[:].bitcast(I32), 0)
        nc.vector.memset(ed_s[:].bitcast(I32), 0)
        nc.vector.memset(ratio[:, I:], 0.0)

        nc.sync.dma_start(et_w[:].bitcast(I32), et_words[0].bitcast(I32))
        nc.sync.dma_start(nodes[:], offs)
        nc.sync.dma_start(ed_w[:].bitcast(I32), ed_words[0].rearrange("p n t -> p (n t)").bitcast(I32))
        nc.sync.dma_start(ht_raw[:], ht.rearrange("(p j) q -> p j q", j=PACK))
        nc.sync.dma_start(hd_raw[:], hd.rearrange("(p j) q -> p j q", j=PACK))
        for quad in range(4):
            for plane, rows in ((et_s, et_scales), (ed_s, ed_scales)):
                nc.sync.dma_start(
                    plane[32 * quad : 32 * quad + 4, :].bitcast(I32),
                    rows[0, 4 * quad : 4 * quad + 4, :].bitcast(I32),
                )
        nc.sync.dma_start(l1_col[:], l1)
        nc.sync.dma_start(l2_col[:], l2)
        nc.sync.dma_start(third_node[:], offs4)
        nc.sync.dma_start(second_node[:], offs3)
        nc.sync.dma_start(first_node[:], offs2)

        h_bf = sb.tile([P, 2, Q, PACK], BF16, name="h_bf", align_bytes=64)
        nc.scalar.activation(h_bf[:, 0], ht_raw[:].rearrange("p j q -> p q j"), ACT.Copy)
        nc.scalar.activation(h_bf[:, 1], hd_raw[:].rearrange("p j q -> p q j"), ACT.Copy, scale=-1.0)
        gap = sb.tile([P, 1], F32, name="gap")
        nc.scalar.activation(gap[:], l2_col[:], ACT.Identity, bias=l1_col[:], scale=-1.0)

        et_wg = sb.tile([P, I], U16, name="et_wg", align_bytes=64)
        ed_wg = sb.tile([P, I], U32, name="ed_wg", align_bytes=64)
        et_sg = sb.tile([P, I], U8, name="et_sg", align_bytes=64)
        ed_sg = sb.tile([P, I], U8, name="ed_sg", align_bytes=64)
        h_w = sb.tile([P, 2 * Q], U32, name="h_w", align_bytes=64)
        h_s = sb.tile([P, 2 * Q], U8, name="h_s", align_bytes=64)

        for lo, hi in ((0, 512), (512, 1024)):
            nc.vector.tensor_copy(et_wg[:, lo:hi], listed(et_w[:], nodes, lo, hi))
        nc.vector.tensor_copy(ed_wg[:], listed(ed_w[:], nodes, 0, I))
        nc.vector.quantize_mx(
            out=h_w[:].bitcast(FP8X4), scales=h_s[:], in_=h_bf[:].rearrange("p a q j -> p (a q j)")
        )
        nc.vector.tensor_copy(et_sg[:], listed(et_s[:], nodes, 0, I))
        for lo in range(0, I, CHUNK):
            nc.vector.tensor_copy(ed_sg[:, lo : lo + CHUNK], listed(ed_s[:], nodes, lo, lo + CHUNK))

        banks = [psum.tile([P, GROUP], F32, name="bank%d" % g) for g in range(I // GROUP)]
        for g, bank in enumerate(banks):
            cols = slice(g * GROUP, (g + 1) * GROUP)
            nc.tensor.matmul_mx(
                out=bank[:], lhsT=h_w[:, :Q].bitcast(FP8X4), lhsT_scale=h_s[:, :Q],
                rhs=et_wg[:, cols].bitcast(FP4X4), rhs_scale=et_sg[:, cols], start=True, stop=False,
            )
        for g, bank in enumerate(banks):
            cols = slice(g * GROUP, (g + 1) * GROUP)
            nc.tensor.matmul_mx(
                out=bank[:], lhsT=h_w[:, Q:].bitcast(FP8X4), lhsT_scale=h_s[:, Q:],
                rhs=ed_wg[:, cols].bitcast(FP8X4), rhs_scale=ed_sg[:, cols], start=False, stop=True,
            )

        for lo in range(0, I, CHUNK):
            log_ratio = ring.tile([P, CHUNK], F32, name="log_ratio")
            parts = [(banks[(lo + c) // GROUP], c) for c in range(0, CHUNK, GROUP)]
            if lo + CHUNK < I:
                for bank, c in parts:
                    nc.scalar.activation(log_ratio[:, c : c + GROUP], bank[:], ACT.Relu, bias=gap[:], scale=-1.0)
                nc.scalar.activation(ratio[:, lo : lo + CHUNK], log_ratio[:], ACT.Exp, scale=-1.0)
            else:
                for bank, c in parts:
                    nc.vector.tensor_scalar(log_ratio[:, c : c + GROUP], bank[:], gap[:], 0.0, ALU.subtract, ALU.min)
                for bank, c in parts:
                    nc.scalar.activation(ratio[:, lo + c : lo + c + GROUP], log_ratio[:, c : c + GROUP], ACT.Exp)

        inner = sb.tile([P, J], F32, name="inner")
        middle = sb.tile([P, J], F32, name="middle")
        outer = sb.tile([P, J - PIECE], F32, name="outer")
        first_tail = sb.tile([P, PIECE], F32, name="first_tail")
        length = sb.tile([P, J], F32, name="length")
        tail = J - PIECE
        nc.vector.tensor_scalar(inner[:], listed(ratio[:], third_node, 0, J), 1.0, 1.0, ALU.mult, ALU.add)
        nc.vector.tensor_copy(first_tail[:], listed(ratio[:, :I], first_node, tail, J))
        for lo in range(0, J, PIECE):
            cols = slice(lo, lo + PIECE)
            nc.vector.tensor_tensor(
                middle[:, cols], listed(ratio[:], second_node, lo, lo + PIECE), inner[:, cols], ALU.mult
            )
            if lo < tail:
                nc.scalar.activation(outer[:, cols], middle[:, cols], ACT.Copy, bias=1.0)
        for lo in range(0, tail, PIECE):
            cols = slice(lo, lo + PIECE)
            nc.vector.tensor_tensor(
                length[:, cols], listed(ratio[:], first_node, lo, lo + PIECE), outer[:, cols], ALU.mult
            )
        nc.vector.scalar_tensor_tensor(length[:, tail:], middle[:, tail:], 1.0, first_tail[:], ALU.add, ALU.mult)
        for lo, hi in ((0, 256), (256, 384), (384, 512)):
            nc.sync.dma_start(out[:, lo:hi], length[:, lo:hi])
